import numpy as np, ml_dtypes
CORES = [4,20,60,84,92,100,116]
N = 7
import mx_ref
NC, KT, WT = 128, 4, 4
BF = ml_dtypes.bfloat16
def cut(t, i, w=512):
    return t[:, w * i:w * i + w]
def pk(c, s, i=0):
    return (np.ascontiguousarray(c[:, 512 * i:512 * i + 512]), mx_ref.live(s[:, 128 * i:128 * i + 128]))
def inputs(rng, e, E):
    def f(*shape):
        v = (rng.standard_normal(shape, dtype=np.float32) * np.exp2(rng.integers(-2, 3, shape[:-1] + (1,)))).astype(BF)
        return mx_ref.spread((v.astype(np.float32) * np.exp2(rng.integers(-E, E + 1, shape[:-2] + (1, 1))).astype(np.float32)).astype(BF), rng, e)
    def packed(k):
        c = np.zeros((N, 128, k * 512), np.uint8); s = np.zeros((N, 128, k * 128), np.uint8)
        for r in range(N):
            for i in range(k):
                a, b = mx_ref.quantize(f(128, 512)); c[r][:, 512 * i:512 * i + 512] = a; s[r][:, 128 * i:128 * i + 128] = mx_ref.plane(b, rng)
        return c, s
    d = {}
    d["wc"], d["ws"] = packed(KT * WT)
    d["x"] = f(N, 128, KT * 4 * NC)
    return d
def setup_inputs(rng):
    return inputs(rng, 0, 0)
def setup_inputs_blocks(rng):
    return inputs(rng, 2, 0)
def setup_inputs_wide(rng):
    d = inputs(rng, 0, 1); d["x"] = inputs(rng, 0, 0)["x"]
    return d
def reference(wc, ws, x):
    X = [[mx_ref.quantize(cut(x[j], t, 4 * NC)) for t in range(KT)] for j in range(N)]
    y = np.zeros((N, 128, N * WT * NC), np.float32)
    for r in range(N):
        for b in range(N * WT):
            j, i = divmod(b, WT)
            for t in range(KT):
                p = mx_ref.matmul(pk(wc[r], ws[r], KT * i + t), X[j][t])
                z = p if t == 0 else z + p
            y[r][:, NC * b:NC * b + NC] = z
    return {"y": y}

@@ -1,0 +1,219 @@
+from concourse.bass import DstId, RemoteDMATransfer
+from concourse.mybir import dt, ActivationFunctionType
+
+N, KT, WT, C = 7, 4, 4, 128
+PAIRS = {1: (1, 2), 2: (3, 4), 3: (5, 6)}
+SIDE = {1: 0, 2: 0, 5: 0, 3: 1, 4: 1, 6: 1}
+
+F8, U8 = "float8_e4m3fn_x4", "uint8"
+SCRATCH = {
+    "raw": ("sbuf", [128, 4 * C], "bfloat16"),
+    "wcb": ("sbuf", [128, WT * C], F8),
+    "wsb": ("sbuf", [128, WT * KT * C], U8),
+    "xc0": ("sbuf", [128, 2 * C], F8), "xs0": ("sbuf", [128, 2 * C], U8),
+    "xc1": ("sbuf", [128, 2 * C], F8), "xs1": ("sbuf", [128, 2 * C], U8),
+    "y0": ("sbuf", [128, 2 * C], "float32"),
+    "y1": ("sbuf", [128, 2 * C], "float32"),
+    "ps": ("psum", [128, 8 * 512], "float32"),
+}
+for _d in range(1, N):
+    for _t in range(KT):
+        SCRATCH["lc%d%d" % (_d, _t)] = ("dram", [128, C], F8)
+        SCRATCH["ls%d%d" % (_d, _t)] = ("dram", [128, C], U8)
+SEMAPHORES = (["xr", "vq", "mm", "ve", "se", "wsl", "w0", "w1", "w2", "w3", "fx0", "fx1", "st0", "st1", "qs0", "qs1", "gs"]
+              + ["q%d" % t for t in range(KT)] + ["ar%d%d" % (p, t) for p in PAIRS for t in range(KT)])
+
+
+def engines(mask, n):
+    bits = [b for b in range(mask.bit_length()) if mask >> b & 1]
+    return sum(1 << b for b in bits[::max(1, len(bits) // n)][:n])
+
+
+def gateways(rank, T, topo):
+    me = T.cores[rank]
+    others = [c for c in T.cores if c != me]
+    near = [c for c in range(128) if topo.chip(c) == topo.chip(me) and c != me and all(topo.may_write(c, o) for o in others)]
+    return [[c for c in near if (topo.die(c) == topo.die(me)) == (side == 0)] for side in (0, 1)]
+
+
+def u8(view):
+    return view.bitcast(dt.uint8)
+
+
+def copies(g, topo, src_core, src, dsts, n, rsem, lsem):
+    ids = []
+    mask = None
+    for c, v in dsts:
+        rid, pid, se = topo.addr(c)
+        ids.append(DstId(rid=rid, pnc=pid))
+        m = topo.mask(src_core, c)
+        mask = m if mask is None else mask & m
+    g.remote_dma_fused([RemoteDMATransfer(dst_ids=ids, dma_engine_mask=engines(mask, n), remote_sem=rsem,
+                                          srcs=[src], dsts=[v for c, v in dsts])], local_sem=lsem)
+
+
+def gateway_program(g, core, T, topo, rank, side, k):
+    S = T.sem
+    mine = [t for t in range(KT) if t % 2 == k]
+    sgroup = 1 if side == 0 else 2
+    late = [d for d in PAIRS[3] if SIDE[d] == side]
+    jobs = [(sgroup, t, list(PAIRS[sgroup])) for t in mine] + [(3, t, late) for t in reversed(mine)]
+    sent = 0
+    ready = set()
+    for p, t, ds in jobs:
+        if t not in ready:
+            g.wait_ge(S["q%d" % t], 16)
+            ready.add(t)
+        for what in ("lc", "ls"):
+            f = u8 if what == "lc" else (lambda v: v)
+            dsts = [(T.cores[(rank + d) % N], f(T["%s%d%d" % (what, d, t)][:])) for d in ds]
+            copies(g, topo, core, f(T["%s1%d" % (what, t)][:]), dsts, 8, S["ar%d%d" % (p, t)], S.gs)
+            sent += 8
+    g.wait_ge(S.gs, sent)
+
+
+def rank_program(g, core, T, topo):
+    rank = T.rank_of(core)
+    if rank is None:
+        for r in range(N):
+            if topo.chip(core) != topo.chip(T.cores[r]):
+                continue
+            gw = gateways(r, T, topo)
+            for side in (0, 1):
+                for k in (0, 1):
+                    if gw[side][k] == core:
+                        gateway_program(g, core, T, topo, r, side, k)
+        return
+    S = T.sem
+    xc, xs, ybuf = [T.xc0, T.xc1], [T.xs0, T.xs1], [T.y0, T.y1]
+    bank0 = {0: 0, 1: 4, 2: 0, 3: 4}
+
+    steps = [(0, t) for t in range(KT)]
+    for t in range(KT):
+        steps += [(1, t), (2, t)]
+    steps += [(3, t) for t in reversed(range(KT))]
+    first, last = {0: 0, 1: 0, 2: 0, 3: KT - 1}, {0: KT - 1, 1: KT - 1, 2: KT - 1, 3: 0}
+    done = {}
+    for p, t in steps:
+        for i in range(WT):
+            done[p, t, i] = len(done) + 1
+
+    def slot(p, t):
+        if p == 0:
+            return t // 2, 0
+        if p < 3:
+            return p - 1, t + 1
+        return (KT - 1 - t) % 2, 5 + (KT - 1 - t) // 2
+
+    wloads = [0, 1, 2, 3, 0, 1, 2, 3, 2, 1, 0]
+    wlast = [(0, 0), (0, 1), (0, 2), (0, 3), (2, 0), (2, 1), (2, 2), (3, 3), (3, 2), (3, 1), (3, 0)]
+    wof = {}
+    for t in range(KT):
+        wof[0, t] = t
+        wof[1, t] = wof[2, t] = 4 + t
+    wof[3, 3] = 7
+    for n, t in enumerate((2, 1, 0)):
+        wof[3, t] = 8 + n
+
+    gw = gateways(rank, T, topo)
+    for t in range(KT):
+        s, h = t // 2, t % 2
+        g.wait_ge(S.vq, t + 1)
+        to = [gw[0][t % 2], gw[1][t % 2]]
+        copies(g, topo, core, u8(xc[s][:, C * h:C * h + C]), [(c, u8(T["lc1%d" % t][:])) for c in to], 8, S["q%d" % t], S["qs%d" % s])
+        copies(g, topo, core, xs[s][:, C * h:C * h + C], [(c, T["ls1%d" % t][:]) for c in to], 8, S["q%d" % t], S["qs%d" % s])
+
+    def wload(n):
+        t = wloads[n]
+        for i in range(WT):
+            if n:
+                p0, t0 = wlast[n - 1]
+                g.sync.wait_ge(S.mm, done[p0, t0, i])
+            k = KT * i + t
+            g.sync.dma_start(u8(T.wcb[:, C * i:C * i + C]), T.wc[:, 512 * k:512 * k + 512]).then_inc(S["w%d" % i], 16)
+
+    def fetch(p, t, free):
+        s, k = slot(p, t)
+        g.sync.wait_ge(S.mm, done[free + (WT - 1,)])
+        if k == 1:
+            g.sync.wait_ge(S["qs%d" % s], 32)
+        g.sync.wait_ge(S["ar%d%d" % (p, t)], 32)
+        for m, d in enumerate(PAIRS[p]):
+            g.sync.dma_start(u8(xc[s][:, C * m:C * m + C]), u8(T["lc%d%d" % (d, t)][:])).then_inc(S["fx%d" % s], 16)
+        for m, d in enumerate(PAIRS[p]):
+            g.sync.dma_start(xs[s][:, C * m:C * m + C], T["ls%d%d" % (d, t)][:]).then_inc(S["fx%d" % s], 16)
+
+    wload(0)
+    g.sync.dma_start(T.wsb[:], T.ws[:, :]).then_inc(S.wsl, 16)
+    for n in range(1, 4):
+        wload(n)
+    for t in range(KT):
+        fetch(1, t, (0, 1) if t == 0 else (1, t - 1))
+        wload(4 + t)
+        fetch(2, t, (0, 3) if t == 0 else (2, t - 1))
+    fetch(3, 3, (1, 3))
+    fetch(3, 2, (2, 3))
+    wload(8)
+    fetch(3, 1, (3, 3))
+    wload(9)
+    fetch(3, 0, (3, 2))
+    wload(10)
+
+    fills = [(0, h, 0) for h in (0, 1)]
+    for p in PAIRS:
+        fills += [(p, h, m) for h in (0, 1) for m in (0, 1)]
+    upto = {}
+    for n, (p, h, m) in enumerate(fills):
+        upto[p, h] = n + 1
+
+    g.tensor.wait_ge(S.wsl, 16)
+    for p, t in steps:
+        s, k = slot(p, t)
+        if p == 0:
+            g.tensor.wait_ge(S.vq, t + 1)
+            a, b = C * (t % 2), C * (t % 2) + C
+        else:
+            g.tensor.wait_ge(S["fx%d" % s], 64 * k)
+            a, b = 0, 2 * C
+        for i in range(WT):
+            if p != 2 and (p, t) != (3, 3):
+                g.tensor.wait_ge(S["w%d" % i], 16 * (wof[p, t] + 1))
+            if p in (2, 3) and t == first[p]:
+                g.tensor.wait_ge(S.se if i % 2 else S.ve, upto[p - 2, i // 2])
+            o = 512 * (bank0[p] + i)
+            w = C * (KT * i + t)
+            g.tensor.matmul_mx(T.ps[:, o:o + b - a], T.wcb[:, C * i:C * i + C], T.wsb[:, w:w + C], xc[s][:, a:b], xs[s][:, a:b],
+                               t == first[p], t == last[p]).then_inc(S.mm, 1)
+
+    for t in range(KT):
+        s, h = t // 2, t % 2
+        g.vector.wait_ge(S.xr, 16 * (t + 1))
+        g.vector.quantize_mx(xc[s][:, C * h:C * h + C], xs[s][:, C * h:C * h + C], T.raw[:]).then_inc(S.vq, 1)
+    for n, (p, h, m) in enumerate(fills):
+        o = 512 * (bank0[p] + 2 * h) + C * m
+        g.vector.wait_ge(S.mm, done[p, last[p], 2 * h])
+        if n >= 2:
+            g.vector.wait_ge(S["st%d" % (n % 2)], 16 * (n // 2))
+        g.vector.tensor_copy(ybuf[n % 2][:, 0:C], T.ps[:, o:o + C]).then_inc(S.ve, 1)
+
+    for t in range(KT):
+        if t:
+            g.scalar.wait_ge(S.vq, t)
+        g.scalar.dma_start(T.raw[:], T.x[:, 512 * t:512 * t + 512]).then_inc(S.xr, 16)
+    for n0 in range(0, len(fills), 2):
+        for n in (n0, n0 + 1):
+            p, h, m = fills[n]
+            o = 512 * (bank0[p] + 2 * h + 1) + C * m
+            g.scalar.wait_ge(S.mm, done[p, last[p], 2 * h + 1])
+            if n >= 2:
+                g.scalar.wait_ge(S["st%d" % (n % 2)], 16 * (n // 2))
+            g.scalar.activation(ybuf[n % 2][:, C:2 * C], T.ps[:, o:o + C], ActivationFunctionType.Copy).then_inc(S.se, 1)
+        for n in (n0, n0 + 1):
+            p, h, m = fills[n]
+            j = rank if p == 0 else (rank - PAIRS[p][m]) % N
+            c = C * (WT * j + 2 * h)
+            g.scalar.wait_ge(S.ve, n + 1)
+            g.scalar.wait_ge(S.se, n + 1)
+            g.scalar.dma_start(T.y[:, c:c + 2 * C], ybuf[n % 2][:]).then_inc(S["st%d" % (n % 2)], 16)
+    for s in (0, 1):
+        g.scalar.wait_ge(S["st%d" % s], 16 * (len(fills) // 2))

@@ -2,26 +2,82 @@ from concourse.bass import DstId, RemoteDMATransfer
 from concourse.mybir import dt, ActivationFunctionType
 
 N, KT, WT, C = 7, 4, 4, 128
-PAIRS = {1: (1, 2), 2: (3, 4), 3: (5, 6)}
-SIDE = {1: 0, 2: 0, 5: 0, 3: 1, 4: 1, 6: 1}
+GROUPS = {1: (1, 2), 2: (3, 4), 3: (5, 6)}
+BANK0 = {0: 0, 1: 4, 2: 0, 3: 4}
+SIDE = {1: 0, 3: 0, 5: 0, 2: 1, 4: 1, 6: 1}
+NW, NY = 4, 2
+
+ORDER = [(0, t, i) for t in range(KT) for i in range(WT)]
+ORDER += [(p, t, i) for t in range(KT) for p in (1, 2) for i in range(WT)]
+ORDER += [(3, t, i) for t in (3, 2) for i in range(WT)]
+ORDER += [(3, 1, 0), (3, 1, 1), (3, 0, 1), (3, 0, 0)] + [(3, t, i) for i in (2, 3) for t in (1, 0)]
+DONE = {k: n + 1 for n, k in enumerate(ORDER)}
+FIRST, LAST, XFIRST, XLAST = {}, {}, {}, {}
+for _p, _t, _i in ORDER:
+    FIRST.setdefault((_p, _i), DONE[_p, _t, _i])
+    LAST[_p, _i] = DONE[_p, _t, _i]
+    XFIRST.setdefault((_p, _t), DONE[_p, _t, _i])
+    XLAST[_p, _t] = DONE[_p, _t, _i]
+
+
+def plan_weights():
+    uses = {}
+    for p, t, i in ORDER:
+        uses.setdefault((i, t), []).append(DONE[p, t, i])
+    where, held, last, count, loads, use = {}, [None] * NW, [0] * NW, [0] * NW, [], {}
+    for p, t, i in ORDER:
+        n = DONE[p, t, i]
+        if (i, t) not in where:
+            def worth(s):
+                later = [u for u in uses[held[s]] if u >= n] if held[s] is not None else []
+                return min(n - last[s] - 1, 4), later[0] if later else 10 ** 6, -last[s]
+            s = max(range(NW), key=worth)
+            if held[s] is not None:
+                del where[held[s]]
+            held[s] = (i, t)
+            where[i, t] = s
+            count[s] += 1
+            loads.append((i, t, s, last[s], n))
+        s = where[i, t]
+        last[s] = n
+        use[n] = (s, count[s])
+    return loads, use
+
+
+def plan_x():
+    free, count, slots, fetches = [XLAST[0, KT - 1], 0], [0, 0], {}, []
+    for p, t in sorted((k for k in XFIRST if k[0]), key=lambda k: XFIRST[k]):
+        s = 0 if free[0] < free[1] else 1
+        if slots:
+            count[s] += 1
+            fetches.append((p, t, s, free[s], XFIRST[p, t]))
+        slots[p, t] = (s, count[s])
+        free[s] = XLAST[p, t]
+    return slots, fetches
+
+
+WLOADS, WUSE = plan_weights()
+XSLOT, FETCHES = plan_x()
+LOADS = sorted([("w",) + l for l in WLOADS] + [("x",) + f for f in FETCHES], key=lambda l: (l[4], l[5]))
+FILLS = [(p, h, m) for _, p, h in sorted((LAST[p, 2 * h + 1], p, h) for p in BANK0 for h in (0, 1)) for m in range(len(GROUPS.get(p, (0,))))]
+UPTO = {(p, h): n + 1 for n, (p, h, m) in enumerate(FILLS)}
 
 F8, U8 = "float8_e4m3fn_x4", "uint8"
 SCRATCH = {
     "raw": ("sbuf", [128, 4 * C], "bfloat16"),
-    "wcb": ("sbuf", [128, WT * C], F8),
+    "wcb": ("sbuf", [128, NW * C], F8),
     "wsb": ("sbuf", [128, WT * KT * C], U8),
-    "xc0": ("sbuf", [128, 2 * C], F8), "xs0": ("sbuf", [128, 2 * C], U8),
-    "xc1": ("sbuf", [128, 2 * C], F8), "xs1": ("sbuf", [128, 2 * C], U8),
-    "y0": ("sbuf", [128, 2 * C], "float32"),
-    "y1": ("sbuf", [128, 2 * C], "float32"),
+    "xcb": ("sbuf", [128, 4 * C], F8),
+    "xsb": ("sbuf", [128, 4 * C], U8),
+    "yb": ("sbuf", [128, NY * 2 * C], "float32"),
     "ps": ("psum", [128, 8 * 512], "float32"),
 }
 for _d in range(1, N):
     for _t in range(KT):
         SCRATCH["lc%d%d" % (_d, _t)] = ("dram", [128, C], F8)
         SCRATCH["ls%d%d" % (_d, _t)] = ("dram", [128, C], U8)
-SEMAPHORES = (["xr", "vq", "mm", "ve", "se", "wsl", "w0", "w1", "w2", "w3", "fx0", "fx1", "st0", "st1", "qs0", "qs1", "gs"]
-              + ["q%d" % t for t in range(KT)] + ["ar%d%d" % (p, t) for p in PAIRS for t in range(KT)])
+SEMAPHORES = (["xr", "vq", "mm", "ve", "se", "wsl", "gs", "fx0", "fx1"] + ["w%d" % s for s in range(NW)] + ["st%d" % y for y in range(NY)]
+              + ["q%d" % t for t in range(KT)] + ["qs%d" % t for t in range(KT)] + ["ar%d%d" % (p, t) for p in GROUPS for t in range(KT)])
 
 
 def engines(mask, n):
@@ -52,22 +108,32 @@ def copies(g, topo, src_core, src, dsts, n, rsem, lsem):
                                           srcs=[src], dsts=[v for c, v in dsts])], local_sem=lsem)
 
 
+def column(p, t, m):
+    return C * (t % 2) if p == 0 else C * (2 * XSLOT[p, t][0] + m)
+
+
 def gateway_program(g, core, T, topo, rank, side, k):
     S = T.sem
-    mine = [t for t in range(KT) if t % 2 == k]
-    sgroup = 1 if side == 0 else 2
-    late = [d for d in PAIRS[3] if SIDE[d] == side]
-    jobs = [(sgroup, t, list(PAIRS[sgroup])) for t in mine] + [(3, t, late) for t in reversed(mine)]
     sent = 0
     ready = set()
-    for p, t, ds in jobs:
+    for p, t in XSLOT:
+        ds = [d for d in GROUPS[p] if SIDE[d] == side]
+        if t % 2 != k or not ds:
+            continue
         if t not in ready:
-            g.wait_ge(S["q%d" % t], 16)
+            g.wait_ge(S["q%d" % t], 32)
             ready.add(t)
-        for what in ("lc", "ls"):
-            f = u8 if what == "lc" else (lambda v: v)
-            dsts = [(T.cores[(rank + d) % N], f(T["%s%d%d" % (what, d, t)][:])) for d in ds]
-            copies(g, topo, core, f(T["%s1%d" % (what, t)][:]), dsts, 8, S["ar%d%d" % (p, t)], S.gs)
+        for codes in (False, True):
+            dsts = []
+            for d in ds:
+                a = column(p, t, GROUPS[p].index(d))
+                if XSLOT[p, t][1]:
+                    v = u8(T["lc%d%d" % (d, t)][:]) if codes else T["ls%d%d" % (d, t)][:]
+                else:
+                    v = u8(T.xcb[:, a:a + C]) if codes else T.xsb[:, a:a + C]
+                dsts.append((T.cores[(rank + d) % N], v))
+            src = u8(T["lc1%d" % t][:]) if codes else T["ls1%d" % t][:]
+            copies(g, topo, core, src, dsts, 8, S["ar%d%d" % (p, t)], S.gs)
             sent += 8
     g.wait_ge(S.gs, sent)
 
@@ -85,135 +151,87 @@ def rank_program(g, core, T, topo):
                         gateway_program(g, core, T, topo, r, side, k)
         return
     S = T.sem
-    xc, xs, ybuf = [T.xc0, T.xc1], [T.xs0, T.xs1], [T.y0, T.y1]
-    bank0 = {0: 0, 1: 4, 2: 0, 3: 4}
-
-    steps = [(0, t) for t in range(KT)]
-    for t in range(KT):
-        steps += [(1, t), (2, t)]
-    steps += [(3, t) for t in reversed(range(KT))]
-    first, last = {0: 0, 1: 0, 2: 0, 3: KT - 1}, {0: KT - 1, 1: KT - 1, 2: KT - 1, 3: 0}
-    done = {}
-    for p, t in steps:
-        for i in range(WT):
-            done[p, t, i] = len(done) + 1
-
-    def slot(p, t):
-        if p == 0:
-            return t // 2, 0
-        if p < 3:
-            return p - 1, t + 1
-        return (KT - 1 - t) % 2, 5 + (KT - 1 - t) // 2
-
-    wloads = [0, 1, 2, 3, 0, 1, 2, 3, 2, 1, 0]
-    wlast = [(0, 0), (0, 1), (0, 2), (0, 3), (2, 0), (2, 1), (2, 2), (3, 3), (3, 2), (3, 1), (3, 0)]
-    wof = {}
-    for t in range(KT):
-        wof[0, t] = t
-        wof[1, t] = wof[2, t] = 4 + t
-    wof[3, 3] = 7
-    for n, t in enumerate((2, 1, 0)):
-        wof[3, t] = 8 + n
 
     gw = gateways(rank, T, topo)
     for t in range(KT):
-        s, h = t // 2, t % 2
+        a = column(0, t, 0)
         g.wait_ge(S.vq, t + 1)
         to = [gw[0][t % 2], gw[1][t % 2]]
-        copies(g, topo, core, u8(xc[s][:, C * h:C * h + C]), [(c, u8(T["lc1%d" % t][:])) for c in to], 8, S["q%d" % t], S["qs%d" % s])
-        copies(g, topo, core, xs[s][:, C * h:C * h + C], [(c, T["ls1%d" % t][:]) for c in to], 8, S["q%d" % t], S["qs%d" % s])
+        copies(g, topo, core, T.xsb[:, a:a + C], [(c, T["ls1%d" % t][:]) for c in to], 16, S["q%d" % t], S["qs%d" % t])
+        copies(g, topo, core, u8(T.xcb[:, a:a + C]), [(c, u8(T["lc1%d" % t][:])) for c in to], 16, S["q%d" % t], S["qs%d" % t])
 
-    def wload(n):
-        t = wloads[n]
-        for i in range(WT):
-            if n:
-                p0, t0 = wlast[n - 1]
-                g.sync.wait_ge(S.mm, done[p0, t0, i])
-            k = KT * i + t
-            g.sync.dma_start(u8(T.wcb[:, C * i:C * i + C]), T.wc[:, 512 * k:512 * k + 512]).then_inc(S["w%d" % i], 16)
-
-    def fetch(p, t, free):
-        s, k = slot(p, t)
-        g.sync.wait_ge(S.mm, done[free + (WT - 1,)])
-        if k == 1:
-            g.sync.wait_ge(S["qs%d" % s], 32)
+    g.sync.dma_start(T.raw[:], T.x[:, 0:512]).then_inc(S.xr, 16)
+    own = True
+    for n, l in enumerate(LOADS):
+        if n == WT:
+            g.sync.dma_start(T.wsb[:], T.ws[:, :]).then_inc(S.wsl, 16)
+        if l[4]:
+            g.sync.wait_ge(S.mm, l[4])
+        s = l[3]
+        if l[0] == "w":
+            k = KT * l[1] + l[2]
+            g.sync.dma_start(u8(T.wcb[:, C * s:C * s + C]), T.wc[:, 512 * k:512 * k + 512]).then_inc(S["w%d" % s], 16)
+            continue
+        p, t = l[1], l[2]
+        if s == 0 and own:
+            own = False
+            for o in (KT - 2, KT - 1):
+                g.sync.wait_ge(S["qs%d" % o], 32)
         g.sync.wait_ge(S["ar%d%d" % (p, t)], 32)
-        for m, d in enumerate(PAIRS[p]):
-            g.sync.dma_start(u8(xc[s][:, C * m:C * m + C]), u8(T["lc%d%d" % (d, t)][:])).then_inc(S["fx%d" % s], 16)
-        for m, d in enumerate(PAIRS[p]):
-            g.sync.dma_start(xs[s][:, C * m:C * m + C], T["ls%d%d" % (d, t)][:]).then_inc(S["fx%d" % s], 16)
-
-    wload(0)
-    g.sync.dma_start(T.wsb[:], T.ws[:, :]).then_inc(S.wsl, 16)
-    for n in range(1, 4):
-        wload(n)
-    for t in range(KT):
-        fetch(1, t, (0, 1) if t == 0 else (1, t - 1))
-        wload(4 + t)
-        fetch(2, t, (0, 3) if t == 0 else (2, t - 1))
-    fetch(3, 3, (1, 3))
-    fetch(3, 2, (2, 3))
-    wload(8)
-    fetch(3, 1, (3, 3))
-    wload(9)
-    fetch(3, 0, (3, 2))
-    wload(10)
-
-    fills = [(0, h, 0) for h in (0, 1)]
-    for p in PAIRS:
-        fills += [(p, h, m) for h in (0, 1) for m in (0, 1)]
-    upto = {}
-    for n, (p, h, m) in enumerate(fills):
-        upto[p, h] = n + 1
+        for m, d in enumerate(GROUPS[p]):
+            a = column(p, t, m)
+            g.sync.dma_start(u8(T.xcb[:, a:a + C]), u8(T["lc%d%d" % (d, t)][:])).then_inc(S["fx%d" % s], 16)
+        for m, d in enumerate(GROUPS[p]):
+            a = column(p, t, m)
+            g.sync.dma_start(T.xsb[:, a:a + C], T["ls%d%d" % (d, t)][:]).then_inc(S["fx%d" % s], 16)
 
     g.tensor.wait_ge(S.wsl, 16)
-    for p, t in steps:
-        s, k = slot(p, t)
-        if p == 0:
-            g.tensor.wait_ge(S.vq, t + 1)
-            a, b = C * (t % 2), C * (t % 2) + C
-        else:
-            g.tensor.wait_ge(S["fx%d" % s], 64 * k)
-            a, b = 0, 2 * C
-        for i in range(WT):
-            if p != 2 and (p, t) != (3, 3):
-                g.tensor.wait_ge(S["w%d" % i], 16 * (wof[p, t] + 1))
-            if p in (2, 3) and t == first[p]:
-                g.tensor.wait_ge(S.se if i % 2 else S.ve, upto[p - 2, i // 2])
-            o = 512 * (bank0[p] + i)
-            w = C * (KT * i + t)
-            g.tensor.matmul_mx(T.ps[:, o:o + b - a], T.wcb[:, C * i:C * i + C], T.wsb[:, w:w + C], xc[s][:, a:b], xs[s][:, a:b],
-                               t == first[p], t == last[p]).then_inc(S.mm, 1)
+    for p, t, i in ORDER:
+        n = DONE[p, t, i]
+        if n == XFIRST[p, t]:
+            if p == 0:
+                g.tensor.wait_ge(S.vq, t + 1)
+            elif XSLOT[p, t][1]:
+                g.tensor.wait_ge(S["fx%d" % XSLOT[p, t][0]], 64 * XSLOT[p, t][1])
+            else:
+                g.tensor.wait_ge(S["ar%d%d" % (p, t)], 32)
+        s, k = WUSE[n]
+        if all(WUSE[u] != (s, k) for u in range(1, n)):
+            g.tensor.wait_ge(S["w%d" % s], 16 * k)
+        if n == FIRST[p, i] and p >= 2:
+            g.tensor.wait_ge(S.se if i % 2 else S.ve, UPTO[p - 2, i // 2])
+        a, width = column(p, t, 0), C if p == 0 else 2 * C
+        o, w = 512 * (BANK0[p] + i), C * (KT * i + t)
+        g.tensor.matmul_mx(T.ps[:, o:o + width], T.wcb[:, C * s:C * s + C], T.wsb[:, w:w + C], T.xcb[:, a:a + width], T.xsb[:, a:a + width],
+                           n == FIRST[p, i], n == LAST[p, i]).then_inc(S.mm, 1)
 
     for t in range(KT):
-        s, h = t // 2, t % 2
+        a = column(0, t, 0)
+        if t >= 2:
+            g.vector.wait_ge(S["qs%d" % (t - 2)], 32)
+            g.vector.wait_ge(S.mm, XLAST[0, t - 2])
         g.vector.wait_ge(S.xr, 16 * (t + 1))
-        g.vector.quantize_mx(xc[s][:, C * h:C * h + C], xs[s][:, C * h:C * h + C], T.raw[:]).then_inc(S.vq, 1)
-    for n, (p, h, m) in enumerate(fills):
-        o = 512 * (bank0[p] + 2 * h) + C * m
-        g.vector.wait_ge(S.mm, done[p, last[p], 2 * h])
-        if n >= 2:
-            g.vector.wait_ge(S["st%d" % (n % 2)], 16 * (n // 2))
-        g.vector.tensor_copy(ybuf[n % 2][:, 0:C], T.ps[:, o:o + C]).then_inc(S.ve, 1)
+        g.vector.quantize_mx(T.xcb[:, a:a + C], T.xsb[:, a:a + C], T.raw[:]).then_inc(S.vq, 1)
+    for n, (p, h, m) in enumerate(FILLS):
+        o, y = 512 * (BANK0[p] + 2 * h) + C * m, n % NY
+        g.vector.wait_ge(S.mm, LAST[p, 2 * h])
+        if n >= NY:
+            g.vector.wait_ge(S["st%d" % y], 16 * (n // NY))
+        g.vector.tensor_copy(T.yb[:, 2 * C * y:2 * C * y + C], T.ps[:, o:o + C]).then_inc(S.ve, 1)
 
-    for t in range(KT):
-        if t:
-            g.scalar.wait_ge(S.vq, t)
+    for t in range(1, KT):
+        g.scalar.wait_ge(S.vq, t)
         g.scalar.dma_start(T.raw[:], T.x[:, 512 * t:512 * t + 512]).then_inc(S.xr, 16)
-    for n0 in range(0, len(fills), 2):
-        for n in (n0, n0 + 1):
-            p, h, m = fills[n]
-            o = 512 * (bank0[p] + 2 * h + 1) + C * m
-            g.scalar.wait_ge(S.mm, done[p, last[p], 2 * h + 1])
-            if n >= 2:
-                g.scalar.wait_ge(S["st%d" % (n % 2)], 16 * (n // 2))
-            g.scalar.activation(ybuf[n % 2][:, C:2 * C], T.ps[:, o:o + C], ActivationFunctionType.Copy).then_inc(S.se, 1)
-        for n in (n0, n0 + 1):
-            p, h, m = fills[n]
-            j = rank if p == 0 else (rank - PAIRS[p][m]) % N
-            c = C * (WT * j + 2 * h)
-            g.scalar.wait_ge(S.ve, n + 1)
-            g.scalar.wait_ge(S.se, n + 1)
-            g.scalar.dma_start(T.y[:, c:c + 2 * C], ybuf[n % 2][:]).then_inc(S["st%d" % (n % 2)], 16)
-    for s in (0, 1):
-        g.scalar.wait_ge(S["st%d" % s], 16 * (len(fills) // 2))
+    for n, (p, h, m) in enumerate(FILLS):
+        o, y = 512 * (BANK0[p] + 2 * h + 1) + C * m, n % NY
+        g.scalar.wait_ge(S.mm, LAST[p, 2 * h + 1])
+        if n >= NY:
+            g.scalar.wait_ge(S["st%d" % y], 16 * (n // NY))
+        g.scalar.activation(T.yb[:, 2 * C * y + C:2 * C * y + 2 * C], T.ps[:, o:o + C], ActivationFunctionType.Copy).then_inc(S.se, 1)
+        j = rank if p == 0 else (rank - GROUPS[p][m]) % N
+        c = C * (WT * j + 2 * h)
+        g.scalar.wait_ge(S.ve, n + 1)
+        g.scalar.wait_ge(S.se, n + 1)
+        g.scalar.dma_start(T.y[:, c:c + 2 * C], T.yb[:, 2 * C * y:2 * C * y + 2 * C]).then_inc(S["st%d" % y], 16)
+    for y in range(NY):
+        g.scalar.wait_ge(S["st%d" % y], 16 * len(range(y, len(FILLS), NY)))

from concourse.bass import DstId, RemoteDMATransfer
from concourse.mybir import dt, ActivationFunctionType

N, KT, WT, C = 7, 4, 4, 128
GROUPS = {1: (1, 2), 2: (3, 4), 3: (5, 6)}
BANK0 = {0: 0, 1: 4, 2: 0, 3: 4}
SIDE = {1: 0, 3: 0, 5: 0, 2: 1, 4: 1, 6: 1}
NW, NY = 4, 2

ORDER = [(0, t, i) for t in range(KT) for i in range(WT)]
ORDER += [(p, t, i) for t in range(KT) for p in (1, 2) for i in range(WT)]
ORDER += [(3, t, i) for t in (3, 2) for i in range(WT)]
ORDER += [(3, 1, 0), (3, 1, 1), (3, 0, 1), (3, 0, 0)] + [(3, t, i) for i in (2, 3) for t in (1, 0)]
DONE = {k: n + 1 for n, k in enumerate(ORDER)}
FIRST, LAST, XFIRST, XLAST = {}, {}, {}, {}
for _p, _t, _i in ORDER:
    FIRST.setdefault((_p, _i), DONE[_p, _t, _i])
    LAST[_p, _i] = DONE[_p, _t, _i]
    XFIRST.setdefault((_p, _t), DONE[_p, _t, _i])
    XLAST[_p, _t] = DONE[_p, _t, _i]


def plan_weights():
    uses = {}
    for p, t, i in ORDER:
        uses.setdefault((i, t), []).append(DONE[p, t, i])
    where, held, last, count, loads, use = {}, [None] * NW, [0] * NW, [0] * NW, [], {}
    for p, t, i in ORDER:
        n = DONE[p, t, i]
        if (i, t) not in where:
            def worth(s):
                later = [u for u in uses[held[s]] if u >= n] if held[s] is not None else []
                return min(n - last[s] - 1, 4), later[0] if later else 10 ** 6, -last[s]
            s = max(range(NW), key=worth)
            if held[s] is not None:
                del where[held[s]]
            held[s] = (i, t)
            where[i, t] = s
            count[s] += 1
            loads.append((i, t, s, last[s], n))
        s = where[i, t]
        last[s] = n
        use[n] = (s, count[s])
    return loads, use


def plan_x():
    free, count, slots, fetches = [XLAST[0, KT - 1], 0], [0, 0], {}, []
    for p, t in sorted((k for k in XFIRST if k[0]), key=lambda k: XFIRST[k]):
        s = 0 if free[0] < free[1] else 1
        if slots:
            count[s] += 1
            fetches.append((p, t, s, free[s], XFIRST[p, t]))
        slots[p, t] = (s, count[s])
        free[s] = XLAST[p, t]
    return slots, fetches


WLOADS, WUSE = plan_weights()
XSLOT, FETCHES = plan_x()
LOADS = sorted([("w",) + l for l in WLOADS] + [("x",) + f for f in FETCHES], key=lambda l: (l[4], l[5]))
FILLS = [(p, h, m) for _, p, h in sorted((LAST[p, 2 * h + 1], p, h) for p in BANK0 for h in (0, 1)) for m in range(len(GROUPS.get(p, (0,))))]
UPTO = {(p, h): n + 1 for n, (p, h, m) in enumerate(FILLS)}

F8, U8 = "float8_e4m3fn_x4", "uint8"
SCRATCH = {
    "raw": ("sbuf", [128, 4 * C], "bfloat16"),
    "wcb": ("sbuf", [128, NW * C], F8),
    "wsb": ("sbuf", [128, WT * KT * C], U8),
    "xcb": ("sbuf", [128, 4 * C], F8),
    "xsb": ("sbuf", [128, 4 * C], U8),
    "yb": ("sbuf", [128, NY * 2 * C], "float32"),
    "ps": ("psum", [128, 8 * 512], "float32"),
}
for _d in range(1, N):
    for _t in range(KT):
        SCRATCH["lc%d%d" % (_d, _t)] = ("dram", [128, C], F8)
        SCRATCH["ls%d%d" % (_d, _t)] = ("dram", [128, C], U8)
SEMAPHORES = (["xr", "vq", "mm", "ve", "se", "wsl", "gs", "fx0", "fx1"] + ["w%d" % s for s in range(NW)] + ["st%d" % y for y in range(NY)]
              + ["q%d" % t for t in range(KT)] + ["qs%d" % t for t in range(KT)] + ["ar%d%d" % (p, t) for p in GROUPS for t in range(KT)])


def engines(mask, n):
    bits = [b for b in range(mask.bit_length()) if mask >> b & 1]
    return sum(1 << b for b in bits[::max(1, len(bits) // n)][:n])


def gateways(rank, T, topo):
    me = T.cores[rank]
    others = [c for c in T.cores if c != me]
    near = [c for c in range(128) if topo.chip(c) == topo.chip(me) and c != me and all(topo.may_write(c, o) for o in others)]
    return [[c for c in near if (topo.die(c) == topo.die(me)) == (side == 0)] for side in (0, 1)]


def u8(view):
    return view.bitcast(dt.uint8)


def copies(g, topo, src_core, src, dsts, n, rsem, lsem):
    ids = []
    mask = None
    for c, v in dsts:
        rid, pid, se = topo.addr(c)
        ids.append(DstId(rid=rid, pnc=pid))
        m = topo.mask(src_core, c)
        mask = m if mask is None else mask & m
    g.remote_dma_fused([RemoteDMATransfer(dst_ids=ids, dma_engine_mask=engines(mask, n), remote_sem=rsem,
                                          srcs=[src], dsts=[v for c, v in dsts])], local_sem=lsem)


def column(p, t, m):
    return C * (t % 2) if p == 0 else C * (2 * XSLOT[p, t][0] + m)


def gateway_program(g, core, T, topo, rank, side, k):
    S = T.sem
    sent = 0
    ready = set()
    for p, t in XSLOT:
        ds = [d for d in GROUPS[p] if SIDE[d] == side]
        if t % 2 != k or not ds:
            continue
        if t not in ready:
            g.wait_ge(S["q%d" % t], 32)
            ready.add(t)
        for codes in (False, True):
            dsts = []
            for d in ds:
                a = column(p, t, GROUPS[p].index(d))
                if XSLOT[p, t][1]:
                    v = u8(T["lc%d%d" % (d, t)][:]) if codes else T["ls%d%d" % (d, t)][:]
                else:
                    v = u8(T.xcb[:, a:a + C]) if codes else T.xsb[:, a:a + C]
                dsts.append((T.cores[(rank + d) % N], v))
            src = u8(T["lc1%d" % t][:]) if codes else T["ls1%d" % t][:]
            copies(g, topo, core, src, dsts, 8, S["ar%d%d" % (p, t)], S.gs)
            sent += 8
    g.wait_ge(S.gs, sent)


def rank_program(g, core, T, topo):
    rank = T.rank_of(core)
    if rank is None:
        for r in range(N):
            if topo.chip(core) != topo.chip(T.cores[r]):
                continue
            gw = gateways(r, T, topo)
            for side in (0, 1):
                for k in (0, 1):
                    if gw[side][k] == core:
                        gateway_program(g, core, T, topo, r, side, k)
        return
    S = T.sem

    gw = gateways(rank, T, topo)
    for t in range(KT):
        a = column(0, t, 0)
        g.wait_ge(S.vq, t + 1)
        to = [gw[0][t % 2], gw[1][t % 2]]
        copies(g, topo, core, T.xsb[:, a:a + C], [(c, T["ls1%d" % t][:]) for c in to], 16, S["q%d" % t], S["qs%d" % t])
        copies(g, topo, core, u8(T.xcb[:, a:a + C]), [(c, u8(T["lc1%d" % t][:])) for c in to], 16, S["q%d" % t], S["qs%d" % t])

    g.sync.dma_start(T.raw[:], T.x[:, 0:512]).then_inc(S.xr, 16)
    own = True
    for n, l in enumerate(LOADS):
        if n == WT:
            g.sync.dma_start(T.wsb[:], T.ws[:, :]).then_inc(S.wsl, 16)
        if l[4]:
            g.sync.wait_ge(S.mm, l[4])
        s = l[3]
        if l[0] == "w":
            k = KT * l[1] + l[2]
            g.sync.dma_start(u8(T.wcb[:, C * s:C * s + C]), T.wc[:, 512 * k:512 * k + 512]).then_inc(S["w%d" % s], 16)
            continue
        p, t = l[1], l[2]
        if s == 0 and own:
            own = False
            for o in (KT - 2, KT - 1):
                g.sync.wait_ge(S["qs%d" % o], 32)
        g.sync.wait_ge(S["ar%d%d" % (p, t)], 32)
        for m, d in enumerate(GROUPS[p]):
            a = column(p, t, m)
            g.sync.dma_start(u8(T.xcb[:, a:a + C]), u8(T["lc%d%d" % (d, t)][:])).then_inc(S["fx%d" % s], 16)
        for m, d in enumerate(GROUPS[p]):
            a = column(p, t, m)
            g.sync.dma_start(T.xsb[:, a:a + C], T["ls%d%d" % (d, t)][:]).then_inc(S["fx%d" % s], 16)

    g.tensor.wait_ge(S.wsl, 16)
    for p, t, i in ORDER:
        n = DONE[p, t, i]
        if n == XFIRST[p, t]:
            if p == 0:
                g.tensor.wait_ge(S.vq, t + 1)
            elif XSLOT[p, t][1]:
                g.tensor.wait_ge(S["fx%d" % XSLOT[p, t][0]], 64 * XSLOT[p, t][1])
            else:
                g.tensor.wait_ge(S["ar%d%d" % (p, t)], 32)
        s, k = WUSE[n]
        if all(WUSE[u] != (s, k) for u in range(1, n)):
            g.tensor.wait_ge(S["w%d" % s], 16 * k)
        if n == FIRST[p, i] and p >= 2:
            g.tensor.wait_ge(S.se if i % 2 else S.ve, UPTO[p - 2, i // 2])
        a, width = column(p, t, 0), C if p == 0 else 2 * C
        o, w = 512 * (BANK0[p] + i), C * (KT * i + t)
        g.tensor.matmul_mx(T.ps[:, o:o + width], T.wcb[:, C * s:C * s + C], T.wsb[:, w:w + C], T.xcb[:, a:a + width], T.xsb[:, a:a + width],
                           n == FIRST[p, i], n == LAST[p, i]).then_inc(S.mm, 1)

    for t in range(KT):
        a = column(0, t, 0)
        if t >= 2:
            g.vector.wait_ge(S["qs%d" % (t - 2)], 32)
            g.vector.wait_ge(S.mm, XLAST[0, t - 2])
        g.vector.wait_ge(S.xr, 16 * (t + 1))
        g.vector.quantize_mx(T.xcb[:, a:a + C], T.xsb[:, a:a + C], T.raw[:]).then_inc(S.vq, 1)
    for n, (p, h, m) in enumerate(FILLS):
        o, y = 512 * (BANK0[p] + 2 * h) + C * m, n % NY
        g.vector.wait_ge(S.mm, LAST[p, 2 * h])
        if n >= NY:
            g.vector.wait_ge(S["st%d" % y], 16 * (n // NY))
        g.vector.tensor_copy(T.yb[:, 2 * C * y:2 * C * y + C], T.ps[:, o:o + C]).then_inc(S.ve, 1)

    for t in range(1, KT):
        g.scalar.wait_ge(S.vq, t)
        g.scalar.dma_start(T.raw[:], T.x[:, 512 * t:512 * t + 512]).then_inc(S.xr, 16)
    for n, (p, h, m) in enumerate(FILLS):
        o, y = 512 * (BANK0[p] + 2 * h + 1) + C * m, n % NY
        g.scalar.wait_ge(S.mm, LAST[p, 2 * h + 1])
        if n >= NY:
            g.scalar.wait_ge(S["st%d" % y], 16 * (n // NY))
        g.scalar.activation(T.yb[:, 2 * C * y + C:2 * C * y + 2 * C], T.ps[:, o:o + C], ActivationFunctionType.Copy).then_inc(S.se, 1)
        j = rank if p == 0 else (rank - GROUPS[p][m]) % N
        c = C * (WT * j + 2 * h)
        g.scalar.wait_ge(S.ve, n + 1)
        g.scalar.wait_ge(S.se, n + 1)
        g.scalar.dma_start(T.y[:, c:c + 2 * C], T.yb[:, 2 * C * y:2 * C * y + 2 * C]).then_inc(S["st%d" % y], 16)
    for y in range(NY):
        g.scalar.wait_ge(S["st%d" % y], 16 * len(range(y, len(FILLS), NY)))
